import numpy as np
import ml_dtypes


def mxq(x, axis, fmt="e4m3"):
    dtype, down = {"e4m3": (ml_dtypes.float8_e4m3fn, 7), "e5m2": (ml_dtypes.float8_e5m2, 14)}[fmt]
    v = np.moveaxis(np.asarray(x, np.float32).astype(ml_dtypes.bfloat16).astype(np.float64), axis, -1)
    blocks = v.reshape(v.shape[:-1] + (-1, 32))
    amax = np.abs(blocks).max(-1, keepdims=True)
    byte = np.maximum(np.where(amax > 0, np.frexp(amax)[1] - 1 + 127, 0) - down, 1)
    scale = np.exp2(byte - 127.0)
    codes = (blocks / scale).astype(np.float32).astype(dtype).astype(np.float64)
    return np.moveaxis((codes * scale).reshape(v.shape), -1, axis)


WIDE = False


def mx_kscale(k):
    if not WIDE:
        return np.ones(k)
    levels = np.array([24, -24, 12, -12, 0])
    if k % 512:
        return np.exp2(np.random.permutation(np.resize(levels, k // 32))).repeat(32)
    a = np.empty((k // 512, 16))
    for p in range(k // 512):
        a[p, :8] = np.random.permutation(np.resize(levels, 8))
        for g in range(8):
            far = levels[np.abs(levels - a[p, g]) >= 10]
            a[p, g + 8] = far[np.random.randint(len(far))]
    return np.exp2(a.ravel()).repeat(32)


def f64(x):
    return np.asarray(x).astype(np.float64)


def striped8(idx):
    return np.concatenate([v.reshape(-1, 16).T for v in idx]).astype(np.uint16)


def unstriped8(offs):
    return np.stack([offs[16 * g:16 * g + 16].T.reshape(-1) for g in range(8)]).astype(np.int64)


E2M1 = np.array([0.0, 0.5, 1.0, 1.5, 2.0, 3.0, 4.0, 6.0, -0.0, -0.5, -1.0, -1.5, -2.0, -3.0, -4.0, -6.0])


def pack_weight(w, fmt):
    k, n = w.shape
    w = f64(np.asarray(w, np.float32).astype(ml_dtypes.bfloat16)).reshape(k // 32, 32, n)
    amax = np.abs(w).max(1)
    if fmt == "e4m3":
        byte = np.frexp(amax)[1] - 1 + 127 - 7
    else:
        mant, ex = np.frexp(amax / 6.0)
        byte = np.where(mant > 0.5, ex, ex - 1) + 127
    byte = np.clip(np.where(amax > 0, byte, 1), 1, 254)
    scaled = (w * np.exp2(127.0 - byte)[:, None, :]).reshape(k, n).astype(np.float32)
    by_word = np.ascontiguousarray(scaled.reshape(k // 512, 128, 4, n).transpose(0, 1, 3, 2))
    if fmt == "e4m3":
        words = by_word.astype(ml_dtypes.float8_e4m3fn).view(np.uint8)
    else:
        c = by_word.astype(ml_dtypes.float4_e2m1fn).view(np.uint8) & 0xF
        words = (c[..., 0::2] | (c[..., 1::2] << 4)).reshape(k // 512, 128, 2 * n)
    return np.ascontiguousarray(words), np.ascontiguousarray(byte.astype(np.uint8).reshape(k // 512, 16, n))


def unpack_weight(words, scales, fmt):
    g, _, n = scales.shape
    words = np.ascontiguousarray(words).reshape(g, 128, n, -1)
    if fmt == "e4m3":
        vals = words.view(ml_dtypes.float8_e4m3fn).astype(np.float64)
    else:
        nib = np.empty((g, 128, n, 4), np.uint8)
        nib[..., 0::2] = words & 0xF
        nib[..., 1::2] = words >> 4
        vals = E2M1[nib]
    vals = vals * np.repeat(np.exp2(scales.astype(np.float64) - 127.0), 8, axis=1)[..., None]
    return vals.transpose(0, 1, 3, 2).reshape(g * 512, n)


def silu(f):
    return f / (1.0 + np.exp(-np.maximum(f, -700.0)))


K, N, T, J = 512, 512, 2048, 512


def setup_inputs():
    n = np.random.standard_normal
    s = mx_kscale(K)[:, None]
    p_w4 = pack_weight(n((K, N)) / np.sqrt(K) / s, "e2m1")
    return {
        "xT": (n((K, T)) * s).astype(np.float32),
        "wgt": np.repeat(np.random.uniform(0.5, 2.0, (8, 2 * J)), 16, axis=0).astype(np.float32),
        "w4_words": p_w4[0],
        "w4_scales": p_w4[1],
        "wd": (0.4 * (n((K, N)) / np.sqrt(K) / s)).astype(np.float32),
        "b": (0.3 * n(N)).astype(np.float32),
        "offs": striped8(np.stack([np.concatenate([np.random.permutation(T)[:J] for _ in range(2)]) for _ in range(8)])),
    }


def reference(xT, wgt, w4_words, w4_scales, wd, b, offs):
    idx = unstriped8(offs)
    rows = np.arange(K)
    xg = f64(wgt)[rows // 4 % 128] * f64(xT)[rows[:, None], idx[rows % 512 // 64]]
    xT_ = mxq(xg, 0, "e4m3").reshape(K, 2, J)
    w4_ = unpack_weight(w4_words, w4_scales, "e2m1")
    wd_ = mxq(f64(wd), 0, "e4m3")
    a0 = w4_.T @ xT_[:, 0] + wd_.T @ xT_[:, 0]
    a1 = w4_.T @ xT_[:, 1] + wd_.T @ xT_[:, 1]
    return silu(np.abs(a0 - a1) + f64(b)[:, None])

@@ -1,0 +1,196 @@
+from contextlib import ExitStack
+
+import concourse.mybir as mybir
+
+K, N, T, J = 512, 512, 2048, 512
+FLOPS = 2 * 2 * 2 * K * N * J
+
+F32 = mybir.dt.float32
+BF16 = mybir.dt.bfloat16
+I32 = mybir.dt.int32
+U32 = mybir.dt.uint32
+U16 = mybir.dt.uint16
+U8 = mybir.dt.uint8
+FP8X4 = mybir.dt.float8_e4m3fn_x4
+FP4X4 = mybir.dt.float4_e2m1fn_x4
+ACT = mybir.ActivationFunctionType
+ALU = mybir.AluOpType
+
+P = 128
+PACK = 4
+PICKS = 2
+NQ = J // P
+NB = N // P
+
+
+def tile_list_dl_span_silu_kernel(tc, xT, wgt, w4_words, w4_scales, wd, b, offs, out):
+    nc = tc.nc
+    with ExitStack() as ctx:
+        keep = ctx.enter_context(tc.tile_pool(name="keep", bufs=1))
+        psum = ctx.enter_context(tc.psum_pool(name="psum", bufs=1))
+
+        offsets = keep.tile([P, PICKS * J // 16], U16, name="offsets")
+        nc.sync.dma_start(offsets[:], offs)
+
+        w4_sc = keep.tile([P, N], U8, name="w4_sc", align_bytes=64)
+        nc.vector.memset(w4_sc[:].bitcast(I32), 0)
+        warm = keep.tile([P, 2], F32, name="warm")
+        nc.vector.memset(warm[:, 0:1], 0.0)
+        nc.scalar.activation(warm[:, 1:2], warm[:, 0:1], ACT.Silu)
+        for q in range(4):
+            nc.scalar.dma_start(w4_sc[32 * q : 32 * q + 4, :].bitcast(I32), w4_scales[0, 4 * q : 4 * q + 4, :].bitcast(I32))
+
+        x_rows = xT.rearrange("(p i) t -> i p t", i=PACK)
+        planes = [keep.tile([P, T], F32, name=f"plane{i}") for i in range(PACK)]
+        weights = [keep.tile([P, J], F32, name=f"weights{c}") for c in range(PICKS)]
+        nc.sync.dma_start(planes[0][:], x_rows[0])
+        nc.sync.dma_start(weights[0][:, 0 : J // 2], wgt[:, 0 : J // 2])
+        nc.sync.dma_start(weights[0][:, J // 2 : J], wgt[:, J // 2 : J])
+        nc.sync.dma_start(weights[1][:], wgt[:, J : 2 * J])
+        for i in range(1, PACK):
+            nc.sync.dma_start(planes[i][:], x_rows[i])
+        wd_rows = wd.rearrange("(p i) n -> p i n", i=PACK)
+        wd_raw = [keep.tile([P, PACK, N // 2], F32, name=f"wd_raw{u}") for u in range(2)]
+        w4 = keep.tile([P, 2 * N], U8, name="w4", align_bytes=64)
+        nc.sync.dma_start(w4[:].bitcast(I32), w4_words[0].bitcast(I32))
+        nc.sync.dma_start(wd_raw[0][:], wd_rows[:, :, 0 : N // 2])
+        nc.sync.dma_start(wd_raw[1][:], wd_rows[:, :, N // 2 : N])
+        bias = keep.tile([P, NB], F32, name="bias")
+        with nc.allow_non_contiguous_dma(reason="bias, one value a partition"):
+            nc.sync.dma_start(bias[:], b.rearrange("(m p) -> p m", p=P))
+
+        picked = {(u, c): keep.tile([P, 2, J], F32, name=f"picked{u}{c}") for u in range(2) for c in range(PICKS)}
+        xb = [keep.tile([P, PICKS, P, PACK], BF16, name=f"xb{q}", align_bytes=64) for q in range(NQ)]
+        x_codes = [keep.tile([P, PICKS * P], U32, name=f"xc{q}", align_bytes=64) for q in range(NQ)]
+        x_sc = [keep.tile([P, PICKS * P], U8, name=f"xs{q}", align_bytes=64) for q in range(NQ)]
+
+        def gather(i, c, j0, j1):
+            m0, m1 = c * J + j0, c * J + j1
+            nc.vector.tensor_tensor(
+                picked[i // 2, c][:, i % 2, j0:j1],
+                planes[i][:].indirect(offsets[:, m0 // 16 : m1 // 16]),
+                weights[c][:, j0:j1],
+                ALU.mult,
+            )
+
+        def weave(u, q, on_scalar):
+            for c in range(PICKS):
+                dst = xb[q][:, c, :, 2 * u : 2 * u + 2]
+                src = picked[u, c][:, :, q * P : (q + 1) * P].rearrange("p t j -> p j t")
+                sign = 1.0 if c == 0 else -1.0
+                if on_scalar:
+                    nc.scalar.activation(dst, src, ACT.Copy, scale=sign)
+                else:
+                    nc.vector.tensor_scalar_mul(dst, src, sign)
+
+        def quantize_x(q):
+            nc.vector.quantize_mx(out=x_codes[q][:].bitcast(FP8X4), scales=x_sc[q][:], in_=xb[q][:].rearrange("p c j t -> p (c j t)"))
+
+        wd_b = [keep.tile([P, N // 2, PACK], BF16, name=f"wd_b{u}", align_bytes=64) for u in range(2)]
+        wd_codes = [keep.tile([P, N // 2], U32, name=f"wd_c{u}", align_bytes=64) for u in range(2)]
+        wd_sc = [keep.tile([P, N // 2], U8, name=f"wd_s{u}", align_bytes=64) for u in range(2)]
+
+        def weave_wd(u, on_scalar):
+            dst = wd_b[u][:].rearrange("p (c e) t -> p c t e", e=4)
+            src = wd_raw[u][:].rearrange("p t (c e) -> p c t e", e=4)
+            if on_scalar:
+                nc.scalar.copy(dst, src)
+            else:
+                nc.vector.tensor_copy(dst, src)
+
+        def quantize_wd(u):
+            nc.vector.quantize_mx(out=wd_codes[u][:].bitcast(FP8X4), scales=wd_sc[u][:], in_=wd_b[u][:].rearrange("p n t -> p (n t)"))
+
+        acc = {(q, u): psum.tile([P, 2, P], F32, name=f"acc{q}{u}") for q in range(NQ) for u in range(2)}
+
+        def base_passes(q, u):
+            for c in range(PICKS):
+                for r in range(2):
+                    m = 2 * u + r
+                    nc.tensor.matmul_mx(
+                        out=acc[q, u][:, r, :],
+                        lhsT=w4[:, 2 * P * m : 2 * P * (m + 1)].bitcast(FP4X4),
+                        lhsT_scale=w4_sc[:, P * m : P * (m + 1)],
+                        rhs=x_codes[q][:, c * P : (c + 1) * P].bitcast(FP8X4),
+                        rhs_scale=x_sc[q][:, c * P : (c + 1) * P],
+                        start=(c == 0 and r == 0),
+                        stop=False,
+                    )
+
+        def change_passes(q, u):
+            for c in range(PICKS):
+                for r in range(2):
+                    nc.tensor.matmul_mx(
+                        out=acc[q, u][:, r, :],
+                        lhsT=wd_codes[u][:, r * P : (r + 1) * P].bitcast(FP8X4),
+                        lhsT_scale=wd_sc[u][:, r * P : (r + 1) * P],
+                        rhs=x_codes[q][:, c * P : (c + 1) * P].bitcast(FP8X4),
+                        rhs_scale=x_sc[q][:, c * P : (c + 1) * P],
+                        start=False,
+                        stop=(c == PICKS - 1 and r == 1),
+                    )
+
+        out_rows = out.rearrange("(m p) j -> p m j", p=P)
+
+        def finish(q, u, abs_on_vector):
+            span = keep.tile([P, 2, P], F32, name=f"span{q}{u}")
+            if abs_on_vector:
+                flipped = keep.tile([P, 2, P], F32, name=f"flipped{q}{u}")
+                nc.vector.tensor_scalar_mul(flipped[:], acc[q, u][:], -1.0)
+                nc.vector.tensor_tensor(span[:], acc[q, u][:], flipped[:], ALU.max)
+            else:
+                nc.scalar.activation(span[:], acc[q, u][:], ACT.Abs)
+            result = keep.tile([P, 2, P], F32, name=f"result{q}{u}")
+            for r in range(2):
+                m = 2 * u + r
+                nc.scalar.activation(result[:, r, :], span[:, r, :], ACT.Silu, bias=bias[:, m : m + 1])
+            nc.sync.dma_start(out_rows[:, 2 * u : 2 * u + 2, q * P : (q + 1) * P], result[:])
+
+        gather(0, 0, 0, J // 2)
+        gather(0, 0, J // 2, J)
+        gather(0, 1, 0, J)
+        for c in range(PICKS):
+            gather(1, c, 0, J)
+        for q in range(NQ):
+            weave(0, q, True)
+        for c in range(PICKS):
+            gather(2, c, 0, J)
+
+        def last_gathers(q):
+            for c in range(PICKS):
+                gather(3, c, q * P, (q + 1) * P)
+
+        last_gathers(0)
+        weave(1, 0, True)
+        last_gathers(1)
+        weave(1, 1, True)
+        quantize_x(0)
+        weave_wd(0, False)
+        weave_wd(1, True)
+        for u in range(2):
+            base_passes(0, u)
+        quantize_x(1)
+        quantize_wd(0)
+        for u in range(2):
+            base_passes(1, u)
+        for q in range(2):
+            change_passes(q, 0)
+            finish(q, 0, False)
+        last_gathers(2)
+        quantize_wd(1)
+        for q in range(2):
+            change_passes(q, 1)
+            finish(q, 1, False)
+        weave(1, 2, False)
+        last_gathers(3)
+        quantize_x(2)
+        weave(1, 3, False)
+        for u in range(2):
+            base_passes(2, u)
+            change_passes(2, u)
+            finish(2, u, False)
+        quantize_x(3)
+        for u in range(2):
+            base_passes(3, u)
+            change_passes(3, u)
+            finish(3, u, True)

@@ -37,20 +37,21 @@ def tile_list_dl_span_silu_kernel(tc, xT, wgt, w4_words, w4_scales, wd, b, offs,
         warm = keep.tile([P, 2], F32, name="warm")
         nc.vector.memset(warm[:, 0:1], 0.0)
         nc.scalar.activation(warm[:, 1:2], warm[:, 0:1], ACT.Silu)
-        for q in range(4):
-            nc.scalar.dma_start(w4_sc[32 * q : 32 * q + 4, :].bitcast(I32), w4_scales[0, 4 * q : 4 * q + 4, :].bitcast(I32))
 
         x_rows = xT.rearrange("(p i) t -> i p t", i=PACK)
         planes = [keep.tile([P, T], F32, name=f"plane{i}") for i in range(PACK)]
         weights = [keep.tile([P, J], F32, name=f"weights{c}") for c in range(PICKS)]
         nc.sync.dma_start(planes[0][:], x_rows[0])
-        nc.sync.dma_start(weights[0][:, 0 : J // 2], wgt[:, 0 : J // 2])
-        nc.sync.dma_start(weights[0][:, J // 2 : J], wgt[:, J // 2 : J])
+        nc.sync.dma_start(weights[0][:, 0:P], wgt[:, 0:P])
+        nc.sync.dma_start(weights[0][:, P:J], wgt[:, P:J])
         nc.sync.dma_start(weights[1][:], wgt[:, J : 2 * J])
-        for i in range(1, PACK):
+        nc.sync.dma_start(planes[1][:], x_rows[1])
+        for q in range(4):
+            nc.sync.dma_start(w4_sc[32 * q : 32 * q + 4, :].bitcast(I32), w4_scales[0, 4 * q : 4 * q + 4, :].bitcast(I32))
+        for i in range(2, PACK):
             nc.sync.dma_start(planes[i][:], x_rows[i])
         wd_rows = wd.rearrange("(p i) n -> p i n", i=PACK)
-        wd_raw = [keep.tile([P, PACK, N // 2], F32, name=f"wd_raw{u}") for u in range(2)]
+        wd_raw = [keep.tile([P, PACK, N // 2], F32, name=f"wd_raw{u}", tag=f"wd_raw{u}", align_bytes=64) for u in range(2)]
         w4 = keep.tile([P, 2 * N], U8, name="w4", align_bytes=64)
         nc.sync.dma_start(w4[:].bitcast(I32), w4_words[0].bitcast(I32))
         nc.sync.dma_start(wd_raw[0][:], wd_rows[:, :, 0 : N // 2])
@@ -59,34 +60,51 @@ def tile_list_dl_span_silu_kernel(tc, xT, wgt, w4_words, w4_scales, wd, b, offs,
         with nc.allow_non_contiguous_dma(reason="bias, one value a partition"):
             nc.sync.dma_start(bias[:], b.rearrange("(m p) -> p m", p=P))
 
-        picked = {(u, c): keep.tile([P, 2, J], F32, name=f"picked{u}{c}") for u in range(2) for c in range(PICKS)}
-        xb = [keep.tile([P, PICKS, P, PACK], BF16, name=f"xb{q}", align_bytes=64) for q in range(NQ)]
-        x_codes = [keep.tile([P, PICKS * P], U32, name=f"xc{q}", align_bytes=64) for q in range(NQ)]
-        x_sc = [keep.tile([P, PICKS * P], U8, name=f"xs{q}", align_bytes=64) for q in range(NQ)]
+        units = [([0], 0, 2 * P), ([1], 0, 2 * P), ([0, 1], 2 * P, P), ([0, 1], 3 * P, P)]
+        early = [keep.tile([P, 2, J], F32, name=f"early{c}") for c in range(PICKS)]
+        shared = keep.tile([P, 6 * P], F32, name="shared", align_bytes=64)
+        late = [keep.tile([P, 4 * P], F32, name=f"late{s}") for s in range(2)] + [shared]
+        xb = [shared[:, 2 * P : 6 * P].bitcast(BF16)]
+        xb = xb + [keep.tile([P, 2 * P * PACK], BF16, name=f"xb{s}", align_bytes=64)[:] for s in range(1, 4)]
+        x_codes = {s: keep.tile([P, 2 * P], U32, name=f"xc{s}", align_bytes=64) for s in (0, 1)}
+        x_sc = [keep.tile([P, 2 * P], U8, name=f"xs{s}", align_bytes=64) for s in range(4)]
 
-        def gather(i, c, j0, j1):
+        def gather(dst, i, c, j0, j1):
             m0, m1 = c * J + j0, c * J + j1
             nc.vector.tensor_tensor(
-                picked[i // 2, c][:, i % 2, j0:j1],
+                dst,
                 planes[i][:].indirect(offsets[:, m0 // 16 : m1 // 16]),
                 weights[c][:, j0:j1],
                 ALU.mult,
             )
 
-        def weave(u, q, on_scalar):
-            for c in range(PICKS):
-                dst = xb[q][:, c, :, 2 * u : 2 * u + 2]
-                src = picked[u, c][:, :, q * P : (q + 1) * P].rearrange("p t j -> p j t")
-                sign = 1.0 if c == 0 else -1.0
-                if on_scalar:
-                    nc.scalar.activation(dst, src, ACT.Copy, scale=sign)
-                else:
-                    nc.vector.tensor_scalar_mul(dst, src, sign)
+        def gather_late(i, s, only=None):
+            picks, j0, width = units[s]
+            for e, c in enumerate(picks):
+                if only is None or c == only:
+                    col = (i - 2) * 2 * P + e * width
+                    gather(late[s][:, col : col + width], i, c, j0, j0 + width)
 
-        def quantize_x(q):
-            nc.vector.quantize_mx(out=x_codes[q][:].bitcast(FP8X4), scales=x_sc[q][:], in_=xb[q][:].rearrange("p c j t -> p (c j t)"))
+        def weave(u, s, c, on_scalar):
+            picks, j0, width = units[s]
+            cols = slice(picks.index(c) * width, (picks.index(c) + 1) * width)
+            if u == 0:
+                src = early[c][:, :, j0 : j0 + width].rearrange("p t j -> p j t")
+            else:
+                src = late[s][:, 0 : 4 * P].rearrange("p (t j) -> p j t", t=2)[:, cols, :]
+            dst = xb[s].rearrange("p (j t) -> p j t", t=PACK)[:, cols, 2 * u : 2 * u + 2]
+            sign = 1.0 if c == 0 else -1.0
+            if on_scalar:
+                nc.scalar.activation(dst, src, ACT.Copy, scale=sign)
+            else:
+                nc.vector.tensor_scalar_mul(dst, src, sign)
 
-        wd_b = [keep.tile([P, N // 2, PACK], BF16, name=f"wd_b{u}", align_bytes=64) for u in range(2)]
+        def quantize_x(s, lo=0, hi=2 * P):
+            nc.vector.quantize_mx(
+                out=x_codes[s][:, lo:hi].bitcast(FP8X4), scales=x_sc[s][:, lo:hi], in_=xb[s][:, lo * PACK : hi * PACK]
+            )
+
+        wd_b = [keep.tile([P, N // 2, PACK], BF16, name=f"wd_b{u}", tag=f"wd_b{u}", align_bytes=64) for u in range(2)]
         wd_codes = [keep.tile([P, N // 2], U32, name=f"wd_c{u}", align_bytes=64) for u in range(2)]
         wd_sc = [keep.tile([P, N // 2], U8, name=f"wd_s{u}", align_bytes=64) for u in range(2)]
 
@@ -101,96 +119,118 @@ def tile_list_dl_span_silu_kernel(tc, xT, wgt, w4_words, w4_scales, wd, b, offs,
         def quantize_wd(u):
             nc.vector.quantize_mx(out=wd_codes[u][:].bitcast(FP8X4), scales=wd_sc[u][:], in_=wd_b[u][:].rearrange("p n t -> p (n t)"))
 
-        acc = {(q, u): psum.tile([P, 2, P], F32, name=f"acc{q}{u}") for q in range(NQ) for u in range(2)}
+        def mx_pass(dst, m, change, s, lo, hi, start=False, stop=False):
+            if change:
+                cols = slice((m % 2) * P, (m % 2 + 1) * P)
+                lhs, lhs_sc = wd_codes[m // 2][:, cols].bitcast(FP8X4), wd_sc[m // 2][:, cols]
+            else:
+                lhs, lhs_sc = w4[:, 2 * P * m : 2 * P * (m + 1)].bitcast(FP4X4), w4_sc[:, P * m : P * (m + 1)]
+            nc.tensor.matmul_mx(
+                out=dst,
+                lhsT=lhs,
+                lhsT_scale=lhs_sc,
+                rhs=x_codes[s][:, lo:hi].bitcast(FP8X4),
+                rhs_scale=x_sc[s][:, lo:hi],
+                start=start,
+                stop=stop,
+            )
 
-        def base_passes(q, u):
-            for c in range(PICKS):
-                for r in range(2):
-                    m = 2 * u + r
-                    nc.tensor.matmul_mx(
-                        out=acc[q, u][:, r, :],
-                        lhsT=w4[:, 2 * P * m : 2 * P * (m + 1)].bitcast(FP4X4),
-                        lhsT_scale=w4_sc[:, P * m : P * (m + 1)],
-                        rhs=x_codes[q][:, c * P : (c + 1) * P].bitcast(FP8X4),
-                        rhs_scale=x_sc[q][:, c * P : (c + 1) * P],
-                        start=(c == 0 and r == 0),
-                        stop=False,
-                    )
+        wide = [psum.tile([P, 2 * P], F32, name=f"wide{m}") for m in range(NB)]
+        narrow = {(s, u): psum.tile([P, 2 * P], F32, name=f"narrow{s}{u}") for s in (2, 3) for u in range(2)}
 
-        def change_passes(q, u):
+        def wide_base(c):
+            for m in range(NB):
+                for e in range(2):
+                    mx_pass(wide[m][:, e * P : (e + 1) * P], m, False, c, e * P, (e + 1) * P, start=(c == 0 and e == 0))
+
+        def wide_change(m):
             for c in range(PICKS):
+                mx_pass(wide[m][:], m, True, c, 0, 2 * P, stop=(c == 1))
+
+        def narrow_passes(s, u, change, picks):
+            for c in picks:
                 for r in range(2):
-                    nc.tensor.matmul_mx(
-                        out=acc[q, u][:, r, :],
-                        lhsT=wd_codes[u][:, r * P : (r + 1) * P].bitcast(FP8X4),
-                        lhsT_scale=wd_sc[u][:, r * P : (r + 1) * P],
-                        rhs=x_codes[q][:, c * P : (c + 1) * P].bitcast(FP8X4),
-                        rhs_scale=x_sc[q][:, c * P : (c + 1) * P],
-                        start=False,
-                        stop=(c == PICKS - 1 and r == 1),
+                    mx_pass(
+                        narrow[s, u][:, r * P : (r + 1) * P],
+                        2 * u + r,
+                        change,
+                        s,
+                        c * P,
+                        (c + 1) * P,
+                        start=(not change and c == 0 and r == 0),
+                        stop=(change and c == 1 and r == 1),
                     )
 
         out_rows = out.rearrange("(m p) j -> p m j", p=P)
 
-        def finish(q, u, abs_on_vector):
-            span = keep.tile([P, 2, P], F32, name=f"span{q}{u}")
+        def finish(acc, name, ms, j0, abs_on_vector):
+            width = 2 * P // len(ms)
+            span = keep.tile([P, 2 * P], F32, name="span" + name)
             if abs_on_vector:
-                flipped = keep.tile([P, 2, P], F32, name=f"flipped{q}{u}")
-                nc.vector.tensor_scalar_mul(flipped[:], acc[q, u][:], -1.0)
-                nc.vector.tensor_tensor(span[:], acc[q, u][:], flipped[:], ALU.max)
+                flipped = keep.tile([P, 2 * P], F32, name="flipped" + name)
+                nc.vector.tensor_scalar_mul(flipped[:], acc[:], -1.0)
+                nc.vector.tensor_tensor(span[:], acc[:], flipped[:], ALU.max)
             else:
-                nc.scalar.activation(span[:], acc[q, u][:], ACT.Abs)
-            result = keep.tile([P, 2, P], F32, name=f"result{q}{u}")
-            for r in range(2):
-                m = 2 * u + r
-                nc.scalar.activation(result[:, r, :], span[:, r, :], ACT.Silu, bias=bias[:, m : m + 1])
-            nc.sync.dma_start(out_rows[:, 2 * u : 2 * u + 2, q * P : (q + 1) * P], result[:])
+                nc.scalar.activation(span[:], acc[:], ACT.Abs)
+            result = keep.tile([P, len(ms), width], F32, name="result" + name)
+            for r, m in enumerate(ms):
+                nc.scalar.activation(result[:, r, :], span[:, r * width : (r + 1) * width], ACT.Silu, bias=bias[:, m : m + 1])
+            nc.sync.dma_start(out_rows[:, ms[0] : ms[-1] + 1, j0 : j0 + width], result[:])
 
-        gather(0, 0, 0, J // 2)
-        gather(0, 0, J // 2, J)
-        gather(0, 1, 0, J)
+        gather(early[0][:, 0, 0:P], 0, 0, 0, P)
+        gather(early[0][:, 0, P:J], 0, 0, P, J)
+        gather(early[1][:, 0, :], 0, 1, 0, J)
         for c in range(PICKS):
-            gather(1, c, 0, J)
-        for q in range(NQ):
-            weave(0, q, True)
-        for c in range(PICKS):
-            gather(2, c, 0, J)
-
-        def last_gathers(q):
-            for c in range(PICKS):
-                gather(3, c, q * P, (q + 1) * P)
-
-        last_gathers(0)
-        weave(1, 0, True)
-        last_gathers(1)
-        weave(1, 1, True)
-        quantize_x(0)
-        weave_wd(0, False)
+            gather(early[c][:, 1, :], 1, c, 0, J)
+            for s in (c, 2, 3):
+                weave(0, s, c, True)
+        for s in range(3):
+            gather_late(2, s)
+        for s in range(2):
+            gather_late(3, s)
+            weave(1, s, s, True)
+        weave_wd(0, True)
         weave_wd(1, True)
-        for u in range(2):
-            base_passes(0, u)
+        quantize_x(0)
+        wide_base(0)
+        gather_late(3, 2)
         quantize_x(1)
+        wide_base(1)
+        for c in range(PICKS):
+            weave(1, 2, c, False)
         quantize_wd(0)
-        for u in range(2):
-            base_passes(1, u)
-        for q in range(2):
-            change_passes(q, 0)
-            finish(q, 0, False)
-        last_gathers(2)
-        quantize_wd(1)
-        for q in range(2):
-            change_passes(q, 1)
-            finish(q, 1, False)
-        weave(1, 2, False)
-        last_gathers(3)
+        for m in range(2):
+            wide_change(m)
+            finish(wide[m], f"w{m}", [m], 0, False)
+        held = keep.tile([P, 2 * P], U32, name="held", tag="wd_raw0", align_bytes=64)
+        x_codes.setdefault(2, held)
         quantize_x(2)
-        weave(1, 3, False)
+        narrow_passes(2, 0, False, [0, 1])
+        narrow_passes(2, 0, True, [0, 1])
+        finish(narrow[2, 0], "n20", [0, 1], 2 * P, False)
+        narrow_passes(2, 1, False, [0, 1])
+        last = keep.tile([P, 4 * P], F32, name="last", tag="wd_b0", align_bytes=64)
+        late.append(last)
+        gather_late(2, 3, 0)
+        gather_late(3, 3, 0)
+        gather_late(2, 3, 1)
+        weave(1, 3, 0, False)
+        gather_late(3, 3, 1)
+        quantize_wd(1)
+        for m in range(2, NB):
+            wide_change(m)
+            finish(wide[m], f"w{m}", [m], 0, False)
+        narrow_passes(2, 1, True, [0, 1])
+        held_last = keep.tile([P, 2 * P], U32, name="held_last", tag="wd_raw1", align_bytes=64)
+        x_codes.setdefault(3, held_last)
+        weave(1, 3, 1, False)
+        quantize_x(3, 0, P)
         for u in range(2):
-            base_passes(2, u)
-            change_passes(2, u)
-            finish(2, u, False)
-        quantize_x(3)
+            narrow_passes(3, u, False, [0])
+            narrow_passes(3, u, True, [0])
+        quantize_x(3, P, 2 * P)
+        finish(narrow[2, 1], "n21", [2, 3], 2 * P, True)
         for u in range(2):
-            base_passes(3, u)
-            change_passes(3, u)
-            finish(3, u, True)
+            narrow_passes(3, u, False, [1])
+            narrow_passes(3, u, True, [1])
+            finish(narrow[3, u], f"n3{u}", [2 * u, 2 * u + 1], 3 * P, u == 0)

@@ -1,6 +1,7 @@
 from contextlib import ExitStack
 
 import concourse.mybir as mybir
+from concourse.masks import make_identity
 
 K, N, T, J = 512, 512, 2048, 512
 FLOPS = 2 * 2 * 2 * K * N * J
@@ -32,6 +33,13 @@ def tile_list_dl_span_silu_kernel(tc, xT, wgt, w4_words, w4_scales, wd, b, offs,
         offsets = keep.tile([P, PICKS * J // 16], U16, name="offsets")
         nc.sync.dma_start(offsets[:], offs)
 
+        rows = keep.tile([P, P], F32, name="rows")
+        nc.sync.dma_start(rows[0:32, :], wgt[:, 3 * P : 7 * P].rearrange("(g r) (s e) -> r g s e", r=16, e=P)[0])
+        nc.vector.memset(rows[32:64, :], 0.0)
+        nc.vector.memset(rows[64:128, :], 0.0)
+        identity = keep.tile([P, P], F32, name="identity")
+        make_identity(nc, identity[:])
+
         w4_sc = keep.tile([P, N], U8, name="w4_sc", align_bytes=64)
         nc.vector.memset(w4_sc[:].bitcast(I32), 0)
         warm = keep.tile([P, 2], F32, name="warm")
@@ -40,11 +48,11 @@ def tile_list_dl_span_silu_kernel(tc, xT, wgt, w4_words, w4_scales, wd, b, offs,
 
         x_rows = xT.rearrange("(p i) t -> i p t", i=PACK)
         planes = [keep.tile([P, T], F32, name=f"plane{i}") for i in range(PACK)]
-        weights = [keep.tile([P, J], F32, name=f"weights{c}") for c in range(PICKS)]
+        weights = keep.tile([P, PICKS * J], F32, name="weights")
         nc.sync.dma_start(planes[0][:], x_rows[0])
-        nc.sync.dma_start(weights[0][:, 0:P], wgt[:, 0:P])
-        nc.sync.dma_start(weights[0][:, P:J], wgt[:, P:J])
-        nc.sync.dma_start(weights[1][:], wgt[:, J : 2 * J])
+        nc.sync.dma_start(weights[:, 0:P], wgt[:, 0:P])
+        nc.sync.dma_start(weights[:, P : 3 * P], wgt[:, P : 3 * P])
+        nc.sync.dma_start(weights[:, 7 * P : 8 * P], wgt[:, 7 * P : 8 * P])
         nc.sync.dma_start(planes[1][:], x_rows[1])
         for q in range(4):
             nc.sync.dma_start(w4_sc[32 * q : 32 * q + 4, :].bitcast(I32), w4_scales[0, 4 * q : 4 * q + 4, :].bitcast(I32))
@@ -74,7 +82,7 @@ def tile_list_dl_span_silu_kernel(tc, xT, wgt, w4_words, w4_scales, wd, b, offs,
             nc.vector.tensor_tensor(
                 dst,
                 planes[i][:].indirect(offsets[:, m0 // 16 : m1 // 16]),
-                weights[c][:, j0:j1],
+                weights[:, m0:m1],
                 ALU.mult,
             )
 
@@ -135,13 +143,22 @@ def tile_list_dl_span_silu_kernel(tc, xT, wgt, w4_words, w4_scales, wd, b, offs,
                 stop=stop,
             )
 
-        wide = [psum.tile([P, 2 * P], F32, name=f"wide{m}") for m in range(NB)]
-        narrow = {(s, u): psum.tile([P, 2 * P], F32, name=f"narrow{s}{u}") for s in (2, 3) for u in range(2)}
+        turned = psum.tile([P, P], F32, name="turned", tag="narrow30")
+        nc.tensor.transpose(turned[:], rows[:], identity[:])
+        for chunks, tag in ((slice(1, 3), "narrow31"), (slice(0, 4, 3), "narrow21")):
+            spread = keep.tile([P, 2, 8, 16], F32, name="spread" + tag)
+            columns = turned[:, 0:32].rearrange("p (g s) -> p s g", s=4)[:, chunks, :]
+            nc.scalar.copy(spread[:], columns.unsqueeze(3).to_broadcast([P, 2, 8, 16]))
+            back = psum.tile([P, 2, P], F32, name="back" + tag, tag=tag)
+            for s in range(2):
+                nc.tensor.transpose(back[:, s, :], spread[:, s].rearrange("p g r -> p (g r)"), identity[:])
+            nc.scalar.copy(weights[:, 3 * P : 7 * P].rearrange("p (s e) -> p s e", e=P)[:, chunks, :], back[:])
 
-        def wide_base(c):
-            for m in range(NB):
-                for e in range(2):
-                    mx_pass(wide[m][:, e * P : (e + 1) * P], m, False, c, e * P, (e + 1) * P, start=(c == 0 and e == 0))
+        wide = [psum.tile([P, 2 * P], F32, name=f"wide{m}") for m in range(NB)]
+        narrow = {(s, u): psum.tile([P, 2 * P], F32, name=f"narrow{s}{u}", tag=f"narrow{s}{u}") for s in (2, 3) for u in range(2)}
+
+        def wide_base(c, m, e):
+            mx_pass(wide[m][:, e * P : (e + 1) * P], m, False, c, e * P, (e + 1) * P, start=(c == 0 and e == 0))
 
         def wide_change(m):
             for c in range(PICKS):
@@ -178,24 +195,35 @@ def tile_list_dl_span_silu_kernel(tc, xT, wgt, w4_words, w4_scales, wd, b, offs,
             nc.sync.dma_start(out_rows[:, ms[0] : ms[-1] + 1, j0 : j0 + width], result[:])
 
         gather(early[0][:, 0, 0:P], 0, 0, 0, P)
-        gather(early[0][:, 0, P:J], 0, 0, P, J)
-        gather(early[1][:, 0, :], 0, 1, 0, J)
+        gather(early[0][:, 0, P : 3 * P], 0, 0, P, 3 * P)
+        gather(early[1][:, 0, 0 : 2 * P], 0, 1, 0, 2 * P)
+        gather(early[1][:, 0, 2 * P : J], 0, 1, 2 * P, J)
+        gather(early[0][:, 0, 3 * P : J], 0, 0, 3 * P, J)
         for c in range(PICKS):
             gather(early[c][:, 1, :], 1, c, 0, J)
             for s in (c, 2, 3):
                 weave(0, s, c, True)
         for s in range(3):
             gather_late(2, s)
-        for s in range(2):
-            gather_late(3, s)
-            weave(1, s, s, True)
+        for e in range(2):
+            gather(late[0][:, (2 + e) * P : (3 + e) * P], 3, 0, e * P, (e + 1) * P)
+            nc.scalar.copy(
+                xb[0].rearrange("p (j t) -> p j t", t=PACK)[:, e * P : (e + 1) * P, 2:4],
+                late[0][:].rearrange("p (t j) -> p j t", t=2)[:, e * P : (e + 1) * P, :],
+            )
+        gather_late(3, 1)
+        weave(1, 1, 1, True)
         weave_wd(0, True)
         weave_wd(1, True)
-        quantize_x(0)
-        wide_base(0)
+        for e in range(2):
+            quantize_x(0, e * P, (e + 1) * P)
+            for m in range(NB):
+                wide_base(0, m, e)
         gather_late(3, 2)
         quantize_x(1)
-        wide_base(1)
+        for m in range(NB):
+            for e in range(2):
+                wide_base(1, m, e)
         for c in range(PICKS):
             weave(1, 2, c, False)
         quantize_wd(0)
@@ -209,22 +237,28 @@ def tile_list_dl_span_silu_kernel(tc, xT, wgt, w4_words, w4_scales, wd, b, offs,
         narrow_passes(2, 0, True, [0, 1])
         finish(narrow[2, 0], "n20", [0, 1], 2 * P, False)
         narrow_passes(2, 1, False, [0, 1])
-        last = keep.tile([P, 4 * P], F32, name="last", tag="wd_b0", align_bytes=64)
-        late.append(last)
-        gather_late(2, 3, 0)
-        gather_late(3, 3, 0)
-        gather_late(2, 3, 1)
-        weave(1, 3, 0, False)
-        gather_late(3, 3, 1)
+        x_codes.setdefault(3, keep.tile([P, 2 * P], U32, name="xc3", align_bytes=64))
+
+        def last_gathers(c, tag):
+            last = keep.tile([P, 2, P], F32, name=f"last{c}", tag=tag, align_bytes=64)
+            for i in (2, 3):
+                gather(last[:, i - 2, :], i, c, 3 * P, J)
+            return last
+
+        def last_weave(c, last):
+            dst = xb[3].rearrange("p (j t) -> p j t", t=PACK)[:, c * P : (c + 1) * P, 2:4]
+            nc.vector.tensor_scalar_mul(dst, last[:].rearrange("p t j -> p j t"), 1.0 if c == 0 else -1.0)
+
+        first_pick = last_gathers(0, "wd_b0")
         quantize_wd(1)
         for m in range(2, NB):
             wide_change(m)
             finish(wide[m], f"w{m}", [m], 0, False)
         narrow_passes(2, 1, True, [0, 1])
-        held_last = keep.tile([P, 2 * P], U32, name="held_last", tag="wd_raw1", align_bytes=64)
-        x_codes.setdefault(3, held_last)
-        weave(1, 3, 1, False)
+        last_weave(0, first_pick)
+        second_pick = last_gathers(1, "wd_raw1")
         quantize_x(3, 0, P)
+        last_weave(1, second_pick)
         for u in range(2):
             narrow_passes(3, u, False, [0])
             narrow_passes(3, u, True, [0])
@@ -233,4 +267,4 @@ def tile_list_dl_span_silu_kernel(tc, xT, wgt, w4_words, w4_scales, wd, b, offs,
         for u in range(2):
             narrow_passes(3, u, False, [1])
             narrow_passes(3, u, True, [1])
-            finish(narrow[3, u], f"n3{u}", [2 * u, 2 * u + 1], 3 * P, u == 0)
+            finish(narrow[3, u], f"n3{u}", [2 * u, 2 * u + 1], 3 * P, False)

from contextlib import ExitStack

import concourse.mybir as mybir
from concourse.masks import make_identity

K, N, T, J = 512, 512, 2048, 512
FLOPS = 2 * 2 * 2 * K * N * J

F32 = mybir.dt.float32
BF16 = mybir.dt.bfloat16
I32 = mybir.dt.int32
U32 = mybir.dt.uint32
U16 = mybir.dt.uint16
U8 = mybir.dt.uint8
FP8X4 = mybir.dt.float8_e4m3fn_x4
FP4X4 = mybir.dt.float4_e2m1fn_x4
ACT = mybir.ActivationFunctionType
ALU = mybir.AluOpType

P = 128
PACK = 4
PICKS = 2
NQ = J // P
NB = N // P


def tile_list_dl_span_silu_kernel(tc, xT, wgt, w4_words, w4_scales, wd, b, offs, out):
    nc = tc.nc
    with ExitStack() as ctx:
        keep = ctx.enter_context(tc.tile_pool(name="keep", bufs=1))
        psum = ctx.enter_context(tc.psum_pool(name="psum", bufs=1))

        offsets = keep.tile([P, PICKS * J // 16], U16, name="offsets")
        nc.sync.dma_start(offsets[:], offs)

        rows = keep.tile([P, P], F32, name="rows")
        nc.sync.dma_start(rows[0:32, :], wgt[:, 3 * P : 7 * P].rearrange("(g r) (s e) -> r g s e", r=16, e=P)[0])
        nc.vector.memset(rows[32:64, :], 0.0)
        nc.vector.memset(rows[64:128, :], 0.0)
        identity = keep.tile([P, P], F32, name="identity")
        make_identity(nc, identity[:])

        w4_sc = keep.tile([P, N], U8, name="w4_sc", align_bytes=64)
        nc.vector.memset(w4_sc[:].bitcast(I32), 0)
        warm = keep.tile([P, 2], F32, name="warm")
        nc.vector.memset(warm[:, 0:1], 0.0)
        nc.scalar.activation(warm[:, 1:2], warm[:, 0:1], ACT.Silu)

        x_rows = xT.rearrange("(p i) t -> i p t", i=PACK)
        planes = [keep.tile([P, T], F32, name=f"plane{i}") for i in range(PACK)]
        weights = keep.tile([P, PICKS * J], F32, name="weights")
        nc.sync.dma_start(planes[0][:], x_rows[0])
        nc.sync.dma_start(weights[:, 0:P], wgt[:, 0:P])
        nc.sync.dma_start(weights[:, P : 3 * P], wgt[:, P : 3 * P])
        nc.sync.dma_start(weights[:, 7 * P : 8 * P], wgt[:, 7 * P : 8 * P])
        nc.sync.dma_start(planes[1][:], x_rows[1])
        for q in range(4):
            nc.sync.dma_start(w4_sc[32 * q : 32 * q + 4, :].bitcast(I32), w4_scales[0, 4 * q : 4 * q + 4, :].bitcast(I32))
        for i in range(2, PACK):
            nc.sync.dma_start(planes[i][:], x_rows[i])
        wd_rows = wd.rearrange("(p i) n -> p i n", i=PACK)
        wd_raw = [keep.tile([P, PACK, N // 2], F32, name=f"wd_raw{u}", tag=f"wd_raw{u}", align_bytes=64) for u in range(2)]
        w4 = keep.tile([P, 2 * N], U8, name="w4", align_bytes=64)
        nc.sync.dma_start(w4[:].bitcast(I32), w4_words[0].bitcast(I32))
        nc.sync.dma_start(wd_raw[0][:], wd_rows[:, :, 0 : N // 2])
        nc.sync.dma_start(wd_raw[1][:], wd_rows[:, :, N // 2 : N])
        bias = keep.tile([P, NB], F32, name="bias")
        with nc.allow_non_contiguous_dma(reason="bias, one value a partition"):
            nc.sync.dma_start(bias[:], b.rearrange("(m p) -> p m", p=P))

        units = [([0], 0, 2 * P), ([1], 0, 2 * P), ([0, 1], 2 * P, P), ([0, 1], 3 * P, P)]
        early = [keep.tile([P, 2, J], F32, name=f"early{c}") for c in range(PICKS)]
        shared = keep.tile([P, 6 * P], F32, name="shared", align_bytes=64)
        late = [keep.tile([P, 4 * P], F32, name=f"late{s}") for s in range(2)] + [shared]
        xb = [shared[:, 2 * P : 6 * P].bitcast(BF16)]
        xb = xb + [keep.tile([P, 2 * P * PACK], BF16, name=f"xb{s}", align_bytes=64)[:] for s in range(1, 4)]
        x_codes = {s: keep.tile([P, 2 * P], U32, name=f"xc{s}", align_bytes=64) for s in (0, 1)}
        x_sc = [keep.tile([P, 2 * P], U8, name=f"xs{s}", align_bytes=64) for s in range(4)]

        def gather(dst, i, c, j0, j1):
            m0, m1 = c * J + j0, c * J + j1
            nc.vector.tensor_tensor(
                dst,
                planes[i][:].indirect(offsets[:, m0 // 16 : m1 // 16]),
                weights[:, m0:m1],
                ALU.mult,
            )

        def gather_late(i, s, only=None):
            picks, j0, width = units[s]
            for e, c in enumerate(picks):
                if only is None or c == only:
                    col = (i - 2) * 2 * P + e * width
                    gather(late[s][:, col : col + width], i, c, j0, j0 + width)

        def weave(u, s, c, on_scalar):
            picks, j0, width = units[s]
            cols = slice(picks.index(c) * width, (picks.index(c) + 1) * width)
            if u == 0:
                src = early[c][:, :, j0 : j0 + width].rearrange("p t j -> p j t")
            else:
                src = late[s][:, 0 : 4 * P].rearrange("p (t j) -> p j t", t=2)[:, cols, :]
            dst = xb[s].rearrange("p (j t) -> p j t", t=PACK)[:, cols, 2 * u : 2 * u + 2]
            sign = 1.0 if c == 0 else -1.0
            if on_scalar:
                nc.scalar.activation(dst, src, ACT.Copy, scale=sign)
            else:
                nc.vector.tensor_scalar_mul(dst, src, sign)

        def quantize_x(s, lo=0, hi=2 * P):
            nc.vector.quantize_mx(
                out=x_codes[s][:, lo:hi].bitcast(FP8X4), scales=x_sc[s][:, lo:hi], in_=xb[s][:, lo * PACK : hi * PACK]
            )

        wd_b = [keep.tile([P, N // 2, PACK], BF16, name=f"wd_b{u}", tag=f"wd_b{u}", align_bytes=64) for u in range(2)]
        wd_codes = [keep.tile([P, N // 2], U32, name=f"wd_c{u}", align_bytes=64) for u in range(2)]
        wd_sc = [keep.tile([P, N // 2], U8, name=f"wd_s{u}", align_bytes=64) for u in range(2)]

        def weave_wd(u, on_scalar):
            dst = wd_b[u][:].rearrange("p (c e) t -> p c t e", e=4)
            src = wd_raw[u][:].rearrange("p t (c e) -> p c t e", e=4)
            if on_scalar:
                nc.scalar.copy(dst, src)
            else:
                nc.vector.tensor_copy(dst, src)

        def quantize_wd(u):
            nc.vector.quantize_mx(out=wd_codes[u][:].bitcast(FP8X4), scales=wd_sc[u][:], in_=wd_b[u][:].rearrange("p n t -> p (n t)"))

        def mx_pass(dst, m, change, s, lo, hi, start=False, stop=False):
            if change:
                cols = slice((m % 2) * P, (m % 2 + 1) * P)
                lhs, lhs_sc = wd_codes[m // 2][:, cols].bitcast(FP8X4), wd_sc[m // 2][:, cols]
            else:
                lhs, lhs_sc = w4[:, 2 * P * m : 2 * P * (m + 1)].bitcast(FP4X4), w4_sc[:, P * m : P * (m + 1)]
            nc.tensor.matmul_mx(
                out=dst,
                lhsT=lhs,
                lhsT_scale=lhs_sc,
                rhs=x_codes[s][:, lo:hi].bitcast(FP8X4),
                rhs_scale=x_sc[s][:, lo:hi],
                start=start,
                stop=stop,
            )

        turned = psum.tile([P, P], F32, name="turned", tag="narrow30")
        nc.tensor.transpose(turned[:], rows[:], identity[:])
        for chunks, tag in ((slice(1, 3), "narrow31"), (slice(0, 4, 3), "narrow21")):
            spread = keep.tile([P, 2, 8, 16], F32, name="spread" + tag)
            columns = turned[:, 0:32].rearrange("p (g s) -> p s g", s=4)[:, chunks, :]
            nc.scalar.copy(spread[:], columns.unsqueeze(3).to_broadcast([P, 2, 8, 16]))
            back = psum.tile([P, 2, P], F32, name="back" + tag, tag=tag)
            for s in range(2):
                nc.tensor.transpose(back[:, s, :], spread[:, s].rearrange("p g r -> p (g r)"), identity[:])
            nc.scalar.copy(weights[:, 3 * P : 7 * P].rearrange("p (s e) -> p s e", e=P)[:, chunks, :], back[:])

        wide = [psum.tile([P, 2 * P], F32, name=f"wide{m}") for m in range(NB)]
        narrow = {(s, u): psum.tile([P, 2 * P], F32, name=f"narrow{s}{u}", tag=f"narrow{s}{u}") for s in (2, 3) for u in range(2)}

        def wide_base(c, m, e):
            mx_pass(wide[m][:, e * P : (e + 1) * P], m, False, c, e * P, (e + 1) * P, start=(c == 0 and e == 0))

        def wide_change(m):
            for c in range(PICKS):
                mx_pass(wide[m][:], m, True, c, 0, 2 * P, stop=(c == 1))

        def narrow_passes(s, u, change, picks):
            for c in picks:
                for r in range(2):
                    mx_pass(
                        narrow[s, u][:, r * P : (r + 1) * P],
                        2 * u + r,
                        change,
                        s,
                        c * P,
                        (c + 1) * P,
                        start=(not change and c == 0 and r == 0),
                        stop=(change and c == 1 and r == 1),
                    )

        out_rows = out.rearrange("(m p) j -> p m j", p=P)

        def finish(acc, name, ms, j0, abs_on_vector):
            width = 2 * P // len(ms)
            span = keep.tile([P, 2 * P], F32, name="span" + name)
            if abs_on_vector:
                flipped = keep.tile([P, 2 * P], F32, name="flipped" + name)
                nc.vector.tensor_scalar_mul(flipped[:], acc[:], -1.0)
                nc.vector.tensor_tensor(span[:], acc[:], flipped[:], ALU.max)
            else:
                nc.scalar.activation(span[:], acc[:], ACT.Abs)
            result = keep.tile([P, len(ms), width], F32, name="result" + name)
            for r, m in enumerate(ms):
                nc.scalar.activation(result[:, r, :], span[:, r * width : (r + 1) * width], ACT.Silu, bias=bias[:, m : m + 1])
            nc.sync.dma_start(out_rows[:, ms[0] : ms[-1] + 1, j0 : j0 + width], result[:])

        gather(early[0][:, 0, 0:P], 0, 0, 0, P)
        gather(early[0][:, 0, P : 3 * P], 0, 0, P, 3 * P)
        gather(early[1][:, 0, 0 : 2 * P], 0, 1, 0, 2 * P)
        gather(early[1][:, 0, 2 * P : J], 0, 1, 2 * P, J)
        gather(early[0][:, 0, 3 * P : J], 0, 0, 3 * P, J)
        for c in range(PICKS):
            gather(early[c][:, 1, :], 1, c, 0, J)
            for s in (c, 2, 3):
                weave(0, s, c, True)
        for s in range(3):
            gather_late(2, s)
        for e in range(2):
            gather(late[0][:, (2 + e) * P : (3 + e) * P], 3, 0, e * P, (e + 1) * P)
            nc.scalar.copy(
                xb[0].rearrange("p (j t) -> p j t", t=PACK)[:, e * P : (e + 1) * P, 2:4],
                late[0][:].rearrange("p (t j) -> p j t", t=2)[:, e * P : (e + 1) * P, :],
            )
        gather_late(3, 1)
        weave(1, 1, 1, True)
        weave_wd(0, True)
        weave_wd(1, True)
        for e in range(2):
            quantize_x(0, e * P, (e + 1) * P)
            for m in range(NB):
                wide_base(0, m, e)
        gather_late(3, 2)
        quantize_x(1)
        for m in range(NB):
            for e in range(2):
                wide_base(1, m, e)
        for c in range(PICKS):
            weave(1, 2, c, False)
        quantize_wd(0)
        for m in range(2):
            wide_change(m)
            finish(wide[m], f"w{m}", [m], 0, False)
        held = keep.tile([P, 2 * P], U32, name="held", tag="wd_raw0", align_bytes=64)
        x_codes.setdefault(2, held)
        quantize_x(2)
        narrow_passes(2, 0, False, [0, 1])
        narrow_passes(2, 0, True, [0, 1])
        finish(narrow[2, 0], "n20", [0, 1], 2 * P, False)
        narrow_passes(2, 1, False, [0, 1])
        x_codes.setdefault(3, keep.tile([P, 2 * P], U32, name="xc3", align_bytes=64))

        def last_gathers(c, tag):
            last = keep.tile([P, 2, P], F32, name=f"last{c}", tag=tag, align_bytes=64)
            for i in (2, 3):
                gather(last[:, i - 2, :], i, c, 3 * P, J)
            return last

        def last_weave(c, last):
            dst = xb[3].rearrange("p (j t) -> p j t", t=PACK)[:, c * P : (c + 1) * P, 2:4]
            nc.vector.tensor_scalar_mul(dst, last[:].rearrange("p t j -> p j t"), 1.0 if c == 0 else -1.0)

        first_pick = last_gathers(0, "wd_b0")
        quantize_wd(1)
        for m in range(2, NB):
            wide_change(m)
            finish(wide[m], f"w{m}", [m], 0, False)
        narrow_passes(2, 1, True, [0, 1])
        last_weave(0, first_pick)
        second_pick = last_gathers(1, "wd_raw1")
        quantize_x(3, 0, P)
        last_weave(1, second_pick)
        for u in range(2):
            narrow_passes(3, u, False, [0])
            narrow_passes(3, u, True, [0])
        quantize_x(3, P, 2 * P)
        finish(narrow[2, 1], "n21", [2, 3], 2 * P, True)
        for u in range(2):
            narrow_passes(3, u, False, [1])
            narrow_passes(3, u, True, [1])
            finish(narrow[3, u], f"n3{u}", [2 * u, 2 * u + 1], 3 * P, False)
